import numpy as np
import ml_dtypes


def mxq(x, axis, fmt="e4m3"):
    dtype, down = {"e4m3": (ml_dtypes.float8_e4m3fn, 7), "e5m2": (ml_dtypes.float8_e5m2, 14)}[fmt]
    v = np.moveaxis(np.asarray(x, np.float32).astype(ml_dtypes.bfloat16).astype(np.float64), axis, -1)
    blocks = v.reshape(v.shape[:-1] + (-1, 32))
    amax = np.abs(blocks).max(-1, keepdims=True)
    byte = np.maximum(np.where(amax > 0, np.frexp(amax)[1] - 1 + 127, 0) - down, 1)
    scale = np.exp2(byte - 127.0)
    codes = (blocks / scale).astype(np.float32).astype(dtype).astype(np.float64)
    return np.moveaxis((codes * scale).reshape(v.shape), -1, axis)


WIDE = False


def mx_kscale(k):
    if not WIDE:
        return np.ones(k)
    levels = np.array([10, -10, 5, -5, 0])
    if k % 512:
        return np.exp2(np.random.permutation(np.resize(levels, k // 32))).repeat(32)
    a = np.empty((k // 512, 16))
    for p in range(k // 512):
        a[p, :8] = np.random.permutation(np.resize(levels, 8))
        for g in range(8):
            far = levels[np.abs(levels - a[p, g]) >= 10]
            a[p, g + 8] = far[np.random.randint(len(far))]
    return np.exp2(a.ravel()).repeat(32)


def f64(x):
    return np.asarray(x).astype(np.float64)


def striped(idx):
    return np.tile(np.asarray(idx).reshape(-1, 16).T, (8, 1)).astype(np.uint16)


def unstriped(offs):
    return offs[:16].T.reshape(-1).astype(np.int64)


E2M1 = np.array([0.0, 0.5, 1.0, 1.5, 2.0, 3.0, 4.0, 6.0, -0.0, -0.5, -1.0, -1.5, -2.0, -3.0, -4.0, -6.0])


def pack_weight(w, fmt):
    k, n = w.shape
    w = f64(np.asarray(w, np.float32).astype(ml_dtypes.bfloat16)).reshape(k // 32, 32, n)
    amax = np.abs(w).max(1)
    if fmt == "e4m3":
        byte = np.frexp(amax)[1] - 1 + 127 - 7
    else:
        mant, ex = np.frexp(amax / 6.0)
        byte = np.where(mant > 0.5, ex, ex - 1) + 127
    byte = np.clip(np.where(amax > 0, byte, 1), 1, 254)
    scaled = (w * np.exp2(127.0 - byte)[:, None, :]).reshape(k, n).astype(np.float32)
    by_word = np.ascontiguousarray(scaled.reshape(k // 512, 128, 4, n).transpose(0, 1, 3, 2))
    if fmt == "e4m3":
        words = by_word.astype(ml_dtypes.float8_e4m3fn).view(np.uint8)
    else:
        c = by_word.astype(ml_dtypes.float4_e2m1fn).view(np.uint8) & 0xF
        words = (c[..., 0::2] | (c[..., 1::2] << 4)).reshape(k // 512, 128, 2 * n)
    return np.ascontiguousarray(words), np.ascontiguousarray(byte.astype(np.uint8).reshape(k // 512, 16, n))


def unpack_weight(words, scales, fmt):
    g, _, n = scales.shape
    words = np.ascontiguousarray(words).reshape(g, 128, n, -1)
    if fmt == "e4m3":
        vals = words.view(ml_dtypes.float8_e4m3fn).astype(np.float64)
    else:
        nib = np.empty((g, 128, n, 4), np.uint8)
        nib[..., 0::2] = words & 0xF
        nib[..., 1::2] = words >> 4
        vals = E2M1[nib]
    vals = vals * np.repeat(np.exp2(scales.astype(np.float64) - 127.0), 8, axis=1)[..., None]
    return vals.transpose(0, 1, 3, 2).reshape(g * 512, n)


D, T, V, I, Q = 512, 4096, 2048, 512, 128


def setup_inputs():
    n = np.random.standard_normal
    idx = np.random.permutation(T)[:V]
    idx2 = np.random.permutation(V)[:I]
    idx3 = np.random.permutation(V)[:I]
    fd = mx_kscale(D)
    vocp = pack_weight(n((D, T)) / fd[:, None], "e2m1")
    return {
        "ht": (n((D, Q)) * 1.0 / np.sqrt(D) * fd[:, None]).astype(np.float32),
        "voc_words": vocp[0],
        "voc_scales": vocp[1],
        "da": (np.random.uniform(0.0, 0.0008, (Q, I))).astype(np.float32),
        "db": (np.random.uniform(0.0, 0.0008, (Q, I))).astype(np.float32),
        "offs": striped(idx),
        "offs2": striped(idx2),
        "offs3": striped(idx3),
    }


def reference(ht, voc_words, voc_scales, da, db, offs, offs2, offs3):
    idx = unstriped(offs)
    idx2 = unstriped(offs2)
    idx3 = unstriped(offs3)
    vocu = unpack_weight(voc_words, voc_scales, "e2m1")
    htq = mxq(f64(ht), 0, "e4m3")
    vocidxg = vocu[:, idx]
    a = htq.T @ vocidxg
    p = np.exp(a - np.max(a, axis=1, keepdims=True))
    fa = np.zeros((Q, V))
    fa[:, idx2] = f64(da)
    u1 = np.maximum(p / np.sum(p, axis=1, keepdims=True) - fa, 0.0)
    fb = np.zeros((Q, V))
    fb[:, idx3] = f64(db)
    u2 = np.maximum(u1 / np.sum(u1, axis=1, keepdims=True) - fb, 0.0)
    y = u2 / np.sum(u2, axis=1, keepdims=True) * 2048.0
    return y

@@ -1,0 +1,175 @@
+from contextlib import ExitStack
+
+import concourse.mybir as mybir
+
+D, T, V, I, Q = 512, 4096, 2048, 512, 128
+FLOPS = 2 * D * Q * V
+
+F32 = mybir.dt.float32
+BF16 = mybir.dt.bfloat16
+I32 = mybir.dt.int32
+U32 = mybir.dt.uint32
+U16 = mybir.dt.uint16
+U8 = mybir.dt.uint8
+FP8X4 = mybir.dt.float8_e4m3fn_x4
+FP4X4 = mybir.dt.float4_e2m1fn_x4
+ALU = mybir.AluOpType
+ACT = mybir.ActivationFunctionType
+AX = mybir.AxisListType
+
+P = 128
+PACK = 4
+BANK = 512
+GATHER = 1024
+PER_COLUMN = 16
+STAGE_WIDTHS = [384, 384, 384, 384, 256, 256]
+STORE_WIDTHS = [256, 512, 640, 640]
+
+
+def spans(widths):
+    starts = [sum(widths[:n]) for n in range(len(widths))]
+    return [slice(s, s + w) for s, w in zip(starts, widths)]
+
+
+def take_off(nc, pool, name, placed, factor, shares):
+    pieces = spans(STAGE_WIDTHS)
+    extra = len(pieces) - 1
+    diff = pool.tile([P, V + extra], F32, name=name + "_diff")
+    left = pool.tile([P, V + extra], F32, name=name + "_left")
+    total = pool.tile([P, 1], F32, name=name + "_total")
+    for n, cols in enumerate(pieces):
+        nc.vector.scalar_tensor_tensor(
+            out=diff[:, cols], in0=placed[:, cols], scalar=factor[:], in1=shares[:, cols], op0=ALU.mult, op1=ALU.add
+        )
+        if n < extra:
+            nc.scalar.activation(
+                out=left[:, cols], in_=diff[:, cols], func=ACT.Relu, accum_out=diff[:, V + n : V + n + 1]
+            )
+        else:
+            wide = slice(cols.start, V + extra)
+            nc.scalar.activation(out=left[:, wide], in_=diff[:, wide], func=ACT.Relu, accum_out=total[:])
+    return left, total
+
+
+def tile_attend_twodrafts_kernel(tc, ht, voc_words, voc_scales, da, db, offs, offs2, offs3, out):
+    nc = tc.nc
+    with ExitStack() as ctx:
+        lists = ctx.enter_context(tc.tile_pool(name="lists", bufs=1))
+        pool = ctx.enter_context(tc.tile_pool(name="pool", bufs=1))
+        psum = ctx.enter_context(tc.psum_pool(name="psum", bufs=1))
+
+        idx = lists.tile([P, V // PER_COLUMN], U16, name="idx")
+        idx2 = lists.tile([P, I // PER_COLUMN], U16, name="idx2")
+        idx3 = lists.tile([P, I // PER_COLUMN], U16, name="idx3")
+
+        warm_in = pool.tile([P, 1], F32, name="warm_in", tag="late_fill")
+        warm_out = pool.tile([P, 1], F32, name="warm_out")
+        nc.gpsimd.memset(warm_in[:], 0.0)
+        nc.scalar.activation(out=warm_out[:], in_=warm_in[:], func=ACT.Exp)
+
+        scales = pool.tile([P, T], U8, name="scales", align_bytes=64)
+        nc.vector.memset(scales[:].bitcast(I32), 0)
+        fa = pool.tile([P, V], F32, name="fa")
+        nc.vector.memset(fa[:], 0.0)
+        fb_neg = pool.tile([P, V], F32, name="fb_neg", tag="late_fill")
+        nc.gpsimd.memset(fb_neg[:], 0.0)
+
+        da_sb = pool.tile([P, I], F32, name="da_sb")
+        db_sb = pool.tile([P, I], F32, name="db_sb")
+        ht_sb = pool.tile([P, PACK, Q], F32, name="ht_sb")
+        words = pool.tile([P, T], U16, name="words", align_bytes=64)
+        nc.sync.dma_start(idx2[:], offs2)
+        nc.sync.dma_start(da_sb[:], da)
+        nc.sync.dma_start(idx[:], offs)
+        nc.sync.dma_start(ht_sb[:], ht.rearrange("(p j) q -> p j q", j=PACK))
+        for quad in range(4):
+            nc.sync.dma_start(
+                scales[32 * quad : 32 * quad + 4, :].bitcast(I32),
+                voc_scales[0, 4 * quad : 4 * quad + 4, :].bitcast(I32),
+            )
+        nc.sync.dma_start(words[:].bitcast(I32), voc_words[0].bitcast(I32))
+        nc.sync.dma_start(idx3[:], offs3)
+        nc.sync.dma_start(db_sb[:], db)
+
+        nc.vector.tensor_copy(fa[:].indirect(idx2[:]), da_sb[:])
+
+        ht_bf = pool.tile([P, Q, PACK], BF16, name="ht_bf", align_bytes=64)
+        nc.scalar.copy(out=ht_bf[:], in_=ht_sb[:].rearrange("p j q -> p q j"))
+        ht_codes = pool.tile([P, Q], U32, name="ht_codes", align_bytes=64)
+        ht_scales = pool.tile([P, Q], U8, name="ht_scales", align_bytes=64)
+        nc.vector.quantize_mx(
+            out=ht_codes[:].bitcast(FP8X4), scales=ht_scales[:], in_=ht_bf[:].rearrange("p q j -> p (q j)")
+        )
+
+        db_neg = pool.tile([P, I], F32, name="db_neg")
+        nc.scalar.activation(out=db_neg[:], in_=db_sb[:], func=ACT.Copy, scale=-1.0)
+
+        listed_words = pool.tile([P, V], U16, name="listed_words", align_bytes=64)
+        listed_scales = pool.tile([P, V], U8, name="listed_scales", align_bytes=64)
+        for start in range(0, V, GATHER):
+            cols = slice(start, start + GATHER)
+            part = idx[:, start // PER_COLUMN : (start + GATHER) // PER_COLUMN]
+            nc.vector.tensor_copy(listed_scales[:, cols], scales[:].indirect(part))
+            nc.vector.tensor_copy(listed_words[:, cols], words[:].indirect(part))
+
+        n_banks = V // BANK
+        banks = [psum.tile([P, BANK], F32, name=f"scores{b}") for b in range(n_banks)]
+        neg_max_parts = pool.tile([P, n_banks], F32, name="neg_max_parts")
+        for b in range(n_banks):
+            cols = slice(b * BANK, (b + 1) * BANK)
+            nc.tensor.matmul_mx(
+                out=banks[b][:],
+                lhsT=ht_codes[:].bitcast(FP8X4),
+                lhsT_scale=ht_scales[:],
+                rhs=listed_words[:, cols].bitcast(FP4X4),
+                rhs_scale=listed_scales[:, cols],
+                start=True,
+                stop=True,
+            )
+            nc.vector.tensor_reduce(
+                out=neg_max_parts[:, b : b + 1], in_=banks[b][:], axis=AX.X, op=ALU.max, negate=True
+            )
+        neg_max = pool.tile([P, 1], F32, name="neg_max")
+        neg_max_copy = pool.tile([P, n_banks], F32, name="neg_max_copy")
+        nc.vector.tensor_scalar(
+            out=neg_max_copy[:],
+            in0=neg_max_parts[:],
+            scalar1=fb_neg[:, 0:1],
+            scalar2=None,
+            op0=ALU.add,
+            op1=ALU.min,
+            accum_out=neg_max[:],
+        )
+        nc.vector.tensor_copy(fb_neg[:].indirect(idx3[:]), db_neg[:])
+
+        p = pool.tile([P, V], F32, name="p")
+        sum_parts = pool.tile([P, n_banks], F32, name="sum_parts")
+        for b in range(n_banks):
+            nc.scalar.activation(
+                out=p[:, b * BANK : (b + 1) * BANK],
+                in_=banks[b][:],
+                func=ACT.Exp,
+                bias=neg_max[:],
+                accum_out=sum_parts[:, b : b + 1],
+            )
+        neg_sum = pool.tile([P, 1], F32, name="neg_sum")
+        neg_sum_parts = pool.tile([P, n_banks], F32, name="neg_sum_parts")
+        nc.scalar.activation(out=neg_sum_parts[:], in_=sum_parts[:], func=ACT.Copy, scale=-1.0, accum_out=neg_sum[:])
+
+        u1, sum1 = take_off(nc, pool, "first", fa, neg_sum, p)
+        u2, sum2 = take_off(nc, pool, "second", fb_neg, sum1, u1)
+
+        inverse = pool.tile([P, 1], F32, name="inverse")
+        nc.vector.reciprocal(out=inverse[:], in_=sum2[:])
+        result = pool.tile([P, V], F32, name="result")
+        for n, cols in enumerate(spans(STORE_WIDTHS)):
+            nc.vector.tensor_scalar(
+                out=result[:, cols],
+                in0=u2[:, cols],
+                scalar1=inverse[:],
+                scalar2=float(V),
+                op0=ALU.mult,
+                op1=ALU.mult,
+            )
+            queue = nc.sync if n % 2 == 0 else nc.scalar
+            queue.dma_start(out[:, cols], result[:, cols])

@@ -20,10 +20,15 @@ AX = mybir.AxisListType
 P = 128
 PACK = 4
 BANK = 512
-GATHER = 1024
 PER_COLUMN = 16
-STAGE_WIDTHS = [384, 384, 384, 384, 256, 256]
-STORE_WIDTHS = [256, 512, 640, 640]
+SPARE = 8
+SCALE_GATHERS = [2048]
+WORD_GATHERS = [1024,1024]
+FIRST_WIDTHS = [384,384,384,384,256,256]
+SECOND_WIDTHS = [384,384,384,384,256,256]
+STORE_WIDTHS = [256,512,640,640]
+DA_PIECES = [256,256]
+DB_EARLY = 416
 
 
 def spans(widths):
@@ -31,8 +36,12 @@ def spans(widths):
     return [slice(s, s + w) for s, w in zip(starts, widths)]
 
 
-def take_off(nc, pool, name, placed, factor, shares):
-    pieces = spans(STAGE_WIDTHS)
+def list_part(offsets, entries):
+    return offsets[:, entries.start // PER_COLUMN : entries.stop // PER_COLUMN]
+
+
+def take_off(nc, pool, name, widths, placed, factor, shares, first_bias):
+    pieces = spans(widths)
     extra = len(pieces) - 1
     diff = pool.tile([P, V + extra], F32, name=name + "_diff")
     left = pool.tile([P, V + extra], F32, name=name + "_left")
@@ -43,7 +52,11 @@ def take_off(nc, pool, name, placed, factor, shares):
         )
         if n < extra:
             nc.scalar.activation(
-                out=left[:, cols], in_=diff[:, cols], func=ACT.Relu, accum_out=diff[:, V + n : V + n + 1]
+                out=left[:, cols],
+                in_=diff[:, cols],
+                func=ACT.Relu,
+                bias=first_bias if n == 0 else 0.0,
+                accum_out=diff[:, V + n : V + n + 1],
             )
         else:
             wide = slice(cols.start, V + extra)
@@ -62,24 +75,23 @@ def tile_attend_twodrafts_kernel(tc, ht, voc_words, voc_scales, da, db, offs, of
         idx2 = lists.tile([P, I // PER_COLUMN], U16, name="idx2")
         idx3 = lists.tile([P, I // PER_COLUMN], U16, name="idx3")
 
-        warm_in = pool.tile([P, 1], F32, name="warm_in", tag="late_fill")
-        warm_out = pool.tile([P, 1], F32, name="warm_out")
-        nc.gpsimd.memset(warm_in[:], 0.0)
-        nc.scalar.activation(out=warm_out[:], in_=warm_in[:], func=ACT.Exp)
-
         scales = pool.tile([P, T], U8, name="scales", align_bytes=64)
         nc.vector.memset(scales[:].bitcast(I32), 0)
         fa = pool.tile([P, V], F32, name="fa")
         nc.vector.memset(fa[:], 0.0)
-        fb_neg = pool.tile([P, V], F32, name="fb_neg", tag="late_fill")
-        nc.gpsimd.memset(fb_neg[:], 0.0)
+        fb_neg = pool.tile([P, V + SPARE], F32, name="fb_neg")
+        nc.vector.memset(fb_neg[:], 0.0)
+        zero = fb_neg[:, V : V + 1]
+        warm = pool.tile([P, 1], F32, name="warm")
+        nc.scalar.activation(out=warm[:], in_=zero, func=ACT.Exp)
 
-        da_sb = pool.tile([P, I], F32, name="da_sb")
+        da_parts = [pool.tile([P, w], F32, name=f"da{n}") for n, w in enumerate(DA_PIECES)]
         db_sb = pool.tile([P, I], F32, name="db_sb")
         ht_sb = pool.tile([P, PACK, Q], F32, name="ht_sb")
         words = pool.tile([P, T], U16, name="words", align_bytes=64)
         nc.sync.dma_start(idx2[:], offs2)
-        nc.sync.dma_start(da_sb[:], da)
+        for part, entries in zip(da_parts, spans(DA_PIECES)):
+            nc.sync.dma_start(part[:], da[:, entries])
         nc.sync.dma_start(idx[:], offs)
         nc.sync.dma_start(ht_sb[:], ht.rearrange("(p j) q -> p j q", j=PACK))
         for quad in range(4):
@@ -91,7 +103,9 @@ def tile_attend_twodrafts_kernel(tc, ht, voc_words, voc_scales, da, db, offs, of
         nc.sync.dma_start(idx3[:], offs3)
         nc.sync.dma_start(db_sb[:], db)
 
-        nc.vector.tensor_copy(fa[:].indirect(idx2[:]), da_sb[:])
+        for part, entries in zip(da_parts, spans(DA_PIECES)):
+            nc.vector.tensor_copy(fa[:].indirect(list_part(idx2, entries)), part[:])
+
 
         ht_bf = pool.tile([P, Q, PACK], BF16, name="ht_bf", align_bytes=64)
         nc.scalar.copy(out=ht_bf[:], in_=ht_sb[:].rearrange("p j q -> p q j"))
@@ -101,16 +115,15 @@ def tile_attend_twodrafts_kernel(tc, ht, voc_words, voc_scales, da, db, offs, of
             out=ht_codes[:].bitcast(FP8X4), scales=ht_scales[:], in_=ht_bf[:].rearrange("p q j -> p (q j)")
         )
 
-        db_neg = pool.tile([P, I], F32, name="db_neg")
-        nc.scalar.activation(out=db_neg[:], in_=db_sb[:], func=ACT.Copy, scale=-1.0)
+        db_half = pool.tile([P, I], F32, name="db_half")
+        nc.scalar.activation(out=db_half[:], in_=db_sb[:], func=ACT.Copy, scale=-0.5)
 
         listed_words = pool.tile([P, V], U16, name="listed_words", align_bytes=64)
         listed_scales = pool.tile([P, V], U8, name="listed_scales", align_bytes=64)
-        for start in range(0, V, GATHER):
-            cols = slice(start, start + GATHER)
-            part = idx[:, start // PER_COLUMN : (start + GATHER) // PER_COLUMN]
-            nc.vector.tensor_copy(listed_scales[:, cols], scales[:].indirect(part))
-            nc.vector.tensor_copy(listed_words[:, cols], words[:].indirect(part))
+        for cols in spans(SCALE_GATHERS):
+            nc.vector.tensor_copy(listed_scales[:, cols], scales[:].indirect(list_part(idx, cols)))
+        for cols in spans(WORD_GATHERS):
+            nc.vector.tensor_copy(listed_words[:, cols], words[:].indirect(list_part(idx, cols)))
 
         n_banks = V // BANK
         banks = [psum.tile([P, BANK], F32, name=f"scores{b}") for b in range(n_banks)]
@@ -134,13 +147,17 @@ def tile_attend_twodrafts_kernel(tc, ht, voc_words, voc_scales, da, db, offs, of
         nc.vector.tensor_scalar(
             out=neg_max_copy[:],
             in0=neg_max_parts[:],
-            scalar1=fb_neg[:, 0:1],
+            scalar1=zero,
             scalar2=None,
             op0=ALU.add,
             op1=ALU.min,
             accum_out=neg_max[:],
         )
-        nc.vector.tensor_copy(fb_neg[:].indirect(idx3[:]), db_neg[:])
+
+        early, late = spans([DB_EARLY, I - DB_EARLY])
+        nc.vector.tensor_tensor(
+            fb_neg[:].indirect(list_part(idx3, early)), db_half[:, early], db_half[:, early], ALU.add
+        )
 
         p = pool.tile([P, V], F32, name="p")
         sum_parts = pool.tile([P, n_banks], F32, name="sum_parts")
@@ -152,12 +169,17 @@ def tile_attend_twodrafts_kernel(tc, ht, voc_words, voc_scales, da, db, offs, of
                 bias=neg_max[:],
                 accum_out=sum_parts[:, b : b + 1],
             )
-        neg_sum = pool.tile([P, 1], F32, name="neg_sum")
+        neg_total = pool.tile([P, 1], F32, name="neg_total")
         neg_sum_parts = pool.tile([P, n_banks], F32, name="neg_sum_parts")
-        nc.scalar.activation(out=neg_sum_parts[:], in_=sum_parts[:], func=ACT.Copy, scale=-1.0, accum_out=neg_sum[:])
+        nc.scalar.activation(out=neg_sum_parts[:], in_=sum_parts[:], func=ACT.Copy, scale=-1.0, accum_out=neg_total[:])
 
-        u1, sum1 = take_off(nc, pool, "first", fa, neg_sum, p)
-        u2, sum2 = take_off(nc, pool, "second", fb_neg, sum1, u1)
+
+        u1, sum1 = take_off(nc, pool, "first", FIRST_WIDTHS, fa, neg_total, p, zero)
+        nc.vector.tensor_tensor(
+            fb_neg[:].indirect(list_part(idx3, late)), db_half[:, late], db_half[:, late], ALU.add
+        )
+
+        u2, sum2 = take_off(nc, pool, "second", SECOND_WIDTHS, fb_neg, sum1, u1, 0.0)
 
         inverse = pool.tile([P, 1], F32, name="inverse")
         nc.vector.reciprocal(out=inverse[:], in_=sum2[:])

@@ -22,10 +22,10 @@ PACK = 4
 BANK = 512
 PER_COLUMN = 16
 SPARE = 8
-SCALE_GATHERS = [2048]
+SCALE_GATHERS = [1024,1024]
 WORD_GATHERS = [1024,1024]
-FIRST_WIDTHS = [384,384,384,384,256,256]
-SECOND_WIDTHS = [384,384,384,384,256,256]
+FIRST_WIDTHS = [288,320,352,352,368,368]
+SECOND_WIDTHS = [288,320,352,352,368,368]
 STORE_WIDTHS = [256,512,640,640]
 DA_PIECES = [256,256]
 DB_EARLY = 416
@@ -75,10 +75,10 @@ def tile_attend_twodrafts_kernel(tc, ht, voc_words, voc_scales, da, db, offs, of
         idx2 = lists.tile([P, I // PER_COLUMN], U16, name="idx2")
         idx3 = lists.tile([P, I // PER_COLUMN], U16, name="idx3")
 
-        scales = pool.tile([P, T], U8, name="scales", align_bytes=64)
-        nc.vector.memset(scales[:].bitcast(I32), 0)
         fa = pool.tile([P, V], F32, name="fa")
         nc.vector.memset(fa[:], 0.0)
+        scales = pool.tile([P, T], U8, name="scales", align_bytes=64)
+        nc.vector.memset(scales[:].bitcast(I32), 0)
         fb_neg = pool.tile([P, V + SPARE], F32, name="fb_neg")
         nc.vector.memset(fb_neg[:], 0.0)
         zero = fb_neg[:, V : V + 1]
@@ -93,13 +93,13 @@ def tile_attend_twodrafts_kernel(tc, ht, voc_words, voc_scales, da, db, offs, of
         for part, entries in zip(da_parts, spans(DA_PIECES)):
             nc.sync.dma_start(part[:], da[:, entries])
         nc.sync.dma_start(idx[:], offs)
+        nc.sync.dma_start(words[:].bitcast(I32), voc_words[0].bitcast(I32))
         nc.sync.dma_start(ht_sb[:], ht.rearrange("(p j) q -> p j q", j=PACK))
         for quad in range(4):
             nc.sync.dma_start(
                 scales[32 * quad : 32 * quad + 4, :].bitcast(I32),
                 voc_scales[0, 4 * quad : 4 * quad + 4, :].bitcast(I32),
             )
-        nc.sync.dma_start(words[:].bitcast(I32), voc_words[0].bitcast(I32))
         nc.sync.dma_start(idx3[:], offs3)
         nc.sync.dma_start(db_sb[:], db)
 
@@ -120,10 +120,10 @@ def tile_attend_twodrafts_kernel(tc, ht, voc_words, voc_scales, da, db, offs, of
 
         listed_words = pool.tile([P, V], U16, name="listed_words", align_bytes=64)
         listed_scales = pool.tile([P, V], U8, name="listed_scales", align_bytes=64)
-        for cols in spans(SCALE_GATHERS):
-            nc.vector.tensor_copy(listed_scales[:, cols], scales[:].indirect(list_part(idx, cols)))
         for cols in spans(WORD_GATHERS):
             nc.vector.tensor_copy(listed_words[:, cols], words[:].indirect(list_part(idx, cols)))
+        for cols in spans(SCALE_GATHERS):
+            nc.vector.tensor_copy(listed_scales[:, cols], scales[:].indirect(list_part(idx, cols)))
 
         n_banks = V // BANK
         banks = [psum.tile([P, BANK], F32, name=f"scores{b}") for b in range(n_banks)]

@@ -24,10 +24,12 @@ PER_COLUMN = 16
 SPARE = 8
 SCALE_GATHERS = [1024,1024]
 WORD_GATHERS = [1024,1024]
-FIRST_WIDTHS = [288,320,352,352,368,368]
-SECOND_WIDTHS = [288,320,352,352,368,368]
+FIRST_WIDTHS = [256,256,256,256,256,256,256,256]
+SECOND_WIDTHS = [256,256,256,256,256,256,256,256]
 STORE_WIDTHS = [256,512,640,640]
-DA_PIECES = [256,256]
+DA_PIECES = [512]
+FA_FILLS = [1023, 1025]
+FB_FILLS = [319,321]
 DB_EARLY = 416
 
 
@@ -76,11 +78,14 @@ def tile_attend_twodrafts_kernel(tc, ht, voc_words, voc_scales, da, db, offs, of
         idx3 = lists.tile([P, I // PER_COLUMN], U16, name="idx3")
 
         fa = pool.tile([P, V], F32, name="fa")
-        nc.vector.memset(fa[:], 0.0)
+        for cols in spans(FA_FILLS):
+            nc.vector.memset(fa[:, cols], 0.0)
         scales = pool.tile([P, T], U8, name="scales", align_bytes=64)
-        nc.vector.memset(scales[:].bitcast(I32), 0)
+        nc.gpsimd.memset(scales[:].bitcast(I32), 0)
         fb_neg = pool.tile([P, V + SPARE], F32, name="fb_neg")
-        nc.vector.memset(fb_neg[:], 0.0)
+        for cols in spans(FB_FILLS):
+            nc.vector.memset(fb_neg[:, cols], 0.0)
+        nc.gpsimd.memset(fb_neg[:, sum(FB_FILLS) :], 0.0)
         zero = fb_neg[:, V : V + 1]
         warm = pool.tile([P, 1], F32, name="warm")
         nc.scalar.activation(out=warm[:], in_=zero, func=ACT.Exp)

from contextlib import ExitStack

import concourse.mybir as mybir

D, T, V, I, Q = 512, 4096, 2048, 512, 128
FLOPS = 2 * D * Q * V

F32 = mybir.dt.float32
BF16 = mybir.dt.bfloat16
I32 = mybir.dt.int32
U32 = mybir.dt.uint32
U16 = mybir.dt.uint16
U8 = mybir.dt.uint8
FP8X4 = mybir.dt.float8_e4m3fn_x4
FP4X4 = mybir.dt.float4_e2m1fn_x4
ALU = mybir.AluOpType
ACT = mybir.ActivationFunctionType
AX = mybir.AxisListType

P = 128
PACK = 4
BANK = 512
PER_COLUMN = 16
SPARE = 8
SCALE_GATHERS = [1024,1024]
WORD_GATHERS = [1024,1024]
FIRST_WIDTHS = [256,256,256,256,256,256,256,256]
SECOND_WIDTHS = [256,256,256,256,256,256,256,256]
STORE_WIDTHS = [256,512,640,640]
DA_PIECES = [512]
FA_FILLS = [1023, 1025]
FB_FILLS = [319,321]
DB_EARLY = 416


def spans(widths):
    starts = [sum(widths[:n]) for n in range(len(widths))]
    return [slice(s, s + w) for s, w in zip(starts, widths)]


def list_part(offsets, entries):
    return offsets[:, entries.start // PER_COLUMN : entries.stop // PER_COLUMN]


def take_off(nc, pool, name, widths, placed, factor, shares, first_bias):
    pieces = spans(widths)
    extra = len(pieces) - 1
    diff = pool.tile([P, V + extra], F32, name=name + "_diff")
    left = pool.tile([P, V + extra], F32, name=name + "_left")
    total = pool.tile([P, 1], F32, name=name + "_total")
    for n, cols in enumerate(pieces):
        nc.vector.scalar_tensor_tensor(
            out=diff[:, cols], in0=placed[:, cols], scalar=factor[:], in1=shares[:, cols], op0=ALU.mult, op1=ALU.add
        )
        if n < extra:
            nc.scalar.activation(
                out=left[:, cols],
                in_=diff[:, cols],
                func=ACT.Relu,
                bias=first_bias if n == 0 else 0.0,
                accum_out=diff[:, V + n : V + n + 1],
            )
        else:
            wide = slice(cols.start, V + extra)
            nc.scalar.activation(out=left[:, wide], in_=diff[:, wide], func=ACT.Relu, accum_out=total[:])
    return left, total


def tile_attend_twodrafts_kernel(tc, ht, voc_words, voc_scales, da, db, offs, offs2, offs3, out):
    nc = tc.nc
    with ExitStack() as ctx:
        lists = ctx.enter_context(tc.tile_pool(name="lists", bufs=1))
        pool = ctx.enter_context(tc.tile_pool(name="pool", bufs=1))
        psum = ctx.enter_context(tc.psum_pool(name="psum", bufs=1))

        idx = lists.tile([P, V // PER_COLUMN], U16, name="idx")
        idx2 = lists.tile([P, I // PER_COLUMN], U16, name="idx2")
        idx3 = lists.tile([P, I // PER_COLUMN], U16, name="idx3")

        fa = pool.tile([P, V], F32, name="fa")
        for cols in spans(FA_FILLS):
            nc.vector.memset(fa[:, cols], 0.0)
        scales = pool.tile([P, T], U8, name="scales", align_bytes=64)
        nc.gpsimd.memset(scales[:].bitcast(I32), 0)
        fb_neg = pool.tile([P, V + SPARE], F32, name="fb_neg")
        for cols in spans(FB_FILLS):
            nc.vector.memset(fb_neg[:, cols], 0.0)
        nc.gpsimd.memset(fb_neg[:, sum(FB_FILLS) :], 0.0)
        zero = fb_neg[:, V : V + 1]
        warm = pool.tile([P, 1], F32, name="warm")
        nc.scalar.activation(out=warm[:], in_=zero, func=ACT.Exp)

        da_parts = [pool.tile([P, w], F32, name=f"da{n}") for n, w in enumerate(DA_PIECES)]
        db_sb = pool.tile([P, I], F32, name="db_sb")
        ht_sb = pool.tile([P, PACK, Q], F32, name="ht_sb")
        words = pool.tile([P, T], U16, name="words", align_bytes=64)
        nc.sync.dma_start(idx2[:], offs2)
        for part, entries in zip(da_parts, spans(DA_PIECES)):
            nc.sync.dma_start(part[:], da[:, entries])
        nc.sync.dma_start(idx[:], offs)
        nc.sync.dma_start(words[:].bitcast(I32), voc_words[0].bitcast(I32))
        nc.sync.dma_start(ht_sb[:], ht.rearrange("(p j) q -> p j q", j=PACK))
        for quad in range(4):
            nc.sync.dma_start(
                scales[32 * quad : 32 * quad + 4, :].bitcast(I32),
                voc_scales[0, 4 * quad : 4 * quad + 4, :].bitcast(I32),
            )
        nc.sync.dma_start(idx3[:], offs3)
        nc.sync.dma_start(db_sb[:], db)

        for part, entries in zip(da_parts, spans(DA_PIECES)):
            nc.vector.tensor_copy(fa[:].indirect(list_part(idx2, entries)), part[:])


        ht_bf = pool.tile([P, Q, PACK], BF16, name="ht_bf", align_bytes=64)
        nc.scalar.copy(out=ht_bf[:], in_=ht_sb[:].rearrange("p j q -> p q j"))
        ht_codes = pool.tile([P, Q], U32, name="ht_codes", align_bytes=64)
        ht_scales = pool.tile([P, Q], U8, name="ht_scales", align_bytes=64)
        nc.vector.quantize_mx(
            out=ht_codes[:].bitcast(FP8X4), scales=ht_scales[:], in_=ht_bf[:].rearrange("p q j -> p (q j)")
        )

        db_half = pool.tile([P, I], F32, name="db_half")
        nc.scalar.activation(out=db_half[:], in_=db_sb[:], func=ACT.Copy, scale=-0.5)

        listed_words = pool.tile([P, V], U16, name="listed_words", align_bytes=64)
        listed_scales = pool.tile([P, V], U8, name="listed_scales", align_bytes=64)
        for cols in spans(WORD_GATHERS):
            nc.vector.tensor_copy(listed_words[:, cols], words[:].indirect(list_part(idx, cols)))
        for cols in spans(SCALE_GATHERS):
            nc.vector.tensor_copy(listed_scales[:, cols], scales[:].indirect(list_part(idx, cols)))

        n_banks = V // BANK
        banks = [psum.tile([P, BANK], F32, name=f"scores{b}") for b in range(n_banks)]
        neg_max_parts = pool.tile([P, n_banks], F32, name="neg_max_parts")
        for b in range(n_banks):
            cols = slice(b * BANK, (b + 1) * BANK)
            nc.tensor.matmul_mx(
                out=banks[b][:],
                lhsT=ht_codes[:].bitcast(FP8X4),
                lhsT_scale=ht_scales[:],
                rhs=listed_words[:, cols].bitcast(FP4X4),
                rhs_scale=listed_scales[:, cols],
                start=True,
                stop=True,
            )
            nc.vector.tensor_reduce(
                out=neg_max_parts[:, b : b + 1], in_=banks[b][:], axis=AX.X, op=ALU.max, negate=True
            )
        neg_max = pool.tile([P, 1], F32, name="neg_max")
        neg_max_copy = pool.tile([P, n_banks], F32, name="neg_max_copy")
        nc.vector.tensor_scalar(
            out=neg_max_copy[:],
            in0=neg_max_parts[:],
            scalar1=zero,
            scalar2=None,
            op0=ALU.add,
            op1=ALU.min,
            accum_out=neg_max[:],
        )

        early, late = spans([DB_EARLY, I - DB_EARLY])
        nc.vector.tensor_tensor(
            fb_neg[:].indirect(list_part(idx3, early)), db_half[:, early], db_half[:, early], ALU.add
        )

        p = pool.tile([P, V], F32, name="p")
        sum_parts = pool.tile([P, n_banks], F32, name="sum_parts")
        for b in range(n_banks):
            nc.scalar.activation(
                out=p[:, b * BANK : (b + 1) * BANK],
                in_=banks[b][:],
                func=ACT.Exp,
                bias=neg_max[:],
                accum_out=sum_parts[:, b : b + 1],
            )
        neg_total = pool.tile([P, 1], F32, name="neg_total")
        neg_sum_parts = pool.tile([P, n_banks], F32, name="neg_sum_parts")
        nc.scalar.activation(out=neg_sum_parts[:], in_=sum_parts[:], func=ACT.Copy, scale=-1.0, accum_out=neg_total[:])


        u1, sum1 = take_off(nc, pool, "first", FIRST_WIDTHS, fa, neg_total, p, zero)
        nc.vector.tensor_tensor(
            fb_neg[:].indirect(list_part(idx3, late)), db_half[:, late], db_half[:, late], ALU.add
        )

        u2, sum2 = take_off(nc, pool, "second", SECOND_WIDTHS, fb_neg, sum1, u1, 0.0)

        inverse = pool.tile([P, 1], F32, name="inverse")
        nc.vector.reciprocal(out=inverse[:], in_=sum2[:])
        result = pool.tile([P, V], F32, name="result")
        for n, cols in enumerate(spans(STORE_WIDTHS)):
            nc.vector.tensor_scalar(
                out=result[:, cols],
                in0=u2[:, cols],
                scalar1=inverse[:],
                scalar2=float(V),
                op0=ALU.mult,
                op1=ALU.mult,
            )
            queue = nc.sync if n % 2 == 0 else nc.scalar
            queue.dma_start(out[:, cols], result[:, cols])
